import numpy as np
import ml_dtypes


def mxq(x, axis, fmt="e4m3"):
    dtype, down = {"e4m3": (ml_dtypes.float8_e4m3fn, 7), "e5m2": (ml_dtypes.float8_e5m2, 14)}[fmt]
    v = np.moveaxis(np.asarray(x, np.float32).astype(ml_dtypes.bfloat16).astype(np.float64), axis, -1)
    blocks = v.reshape(v.shape[:-1] + (-1, 32))
    amax = np.abs(blocks).max(-1, keepdims=True)
    byte = np.maximum(np.where(amax > 0, np.frexp(amax)[1] - 1 + 127, 0) - down, 1)
    scale = np.exp2(byte - 127.0)
    codes = (blocks / scale).astype(np.float32).astype(dtype).astype(np.float64)
    return np.moveaxis((codes * scale).reshape(v.shape), -1, axis)


WIDE = False


def mx_kscale(k):
    if not WIDE:
        return np.ones(k)
    levels = np.array([30, -30])
    if k % 512:
        return np.exp2(np.random.permutation(np.resize(levels, k // 32))).repeat(32)
    a = np.empty((k // 512, 16))
    for p in range(k // 512):
        a[p, :8] = np.random.permutation(np.resize(levels, 8))
        for g in range(8):
            far = levels[np.abs(levels - a[p, g]) >= 10]
            a[p, g + 8] = far[np.random.randint(len(far))]
    return np.exp2(a.ravel()).repeat(32)


def f64(x):
    return np.asarray(x).astype(np.float64)


def striped(idx):
    return np.tile(np.asarray(idx).reshape(-1, 16).T, (8, 1)).astype(np.uint16)


def unstriped(offs):
    return offs[:16].T.reshape(-1).astype(np.int64)


E2M1 = np.array([0.0, 0.5, 1.0, 1.5, 2.0, 3.0, 4.0, 6.0, -0.0, -0.5, -1.0, -1.5, -2.0, -3.0, -4.0, -6.0])


def pack_weight(w, fmt):
    k, n = w.shape
    w = f64(np.asarray(w, np.float32).astype(ml_dtypes.bfloat16)).reshape(k // 32, 32, n)
    amax = np.abs(w).max(1)
    if fmt in ("e4m3", "e5m2"):
        byte = np.frexp(amax)[1] - 1 + 127 - (7 if fmt == "e4m3" else 14)
    else:
        mant, ex = np.frexp(amax / 6.0)
        byte = np.where(mant > 0.5, ex, ex - 1) + 127
    byte = np.clip(np.where(amax > 0, byte, 1), 1, 254)
    scaled = (w * np.exp2(127.0 - byte)[:, None, :]).reshape(k, n).astype(np.float32)
    by_word = np.ascontiguousarray(scaled.reshape(k // 512, 128, 4, n).transpose(0, 1, 3, 2))
    if fmt in ("e4m3", "e5m2"):
        words = by_word.astype(ml_dtypes.float8_e4m3fn if fmt == "e4m3" else ml_dtypes.float8_e5m2).view(np.uint8)
    else:
        c = by_word.astype(ml_dtypes.float4_e2m1fn).view(np.uint8) & 0xF
        words = (c[..., 0::2] | (c[..., 1::2] << 4)).reshape(k // 512, 128, 2 * n)
    return np.ascontiguousarray(words), np.ascontiguousarray(byte.astype(np.uint8).reshape(k // 512, 16, n))


def unpack_weight(words, scales, fmt):
    g, _, n = scales.shape
    words = np.ascontiguousarray(words).reshape(g, 128, n, -1)
    if fmt in ("e4m3", "e5m2"):
        vals = words.view(ml_dtypes.float8_e4m3fn if fmt == "e4m3" else ml_dtypes.float8_e5m2).astype(np.float64)
    else:
        nib = np.empty((g, 128, n, 4), np.uint8)
        nib[..., 0::2] = words & 0xF
        nib[..., 1::2] = words >> 4
        vals = E2M1[nib]
    vals = vals * np.repeat(np.exp2(scales.astype(np.float64) - 127.0), 8, axis=1)[..., None]
    return vals.transpose(0, 1, 3, 2).reshape(g * 512, n)


def sigmoid(v):
    return 1.0 / (1.0 + np.exp(-v))


K, T, Z, J, R, Q, N, L = 512, 1024, 1024, 256, 512, 1024, 256, 512


def setup_inputs():
    n = np.random.standard_normal
    idx = np.random.permutation(T)[:J]
    idx2 = np.random.permutation(Z)[:J]
    idx3 = np.random.permutation(Q)[:J]
    fk = mx_kscale(K)
    fr = mx_kscale(R)
    fl = mx_kscale(L)
    xtp = pack_weight(n((K, T)) / fk[:, None], "e4m3")
    xop = pack_weight(n((K, Z)) / fk[:, None], "e2m1")
    wp = pack_weight(n((K, R)) * 1 / np.sqrt(K) * fk[:, None] * fr, "e5m2")
    wbp = pack_weight(n((R, N)) * 1 / np.sqrt(R) / fr[:, None], "e5m2")
    sxp = pack_weight(n((L, J)) / fl[:, None], "e2m1")
    wsp = pack_weight(n((L, N)) * 1 / np.sqrt(L) * fl[:, None], "e5m2")
    return {
        "xt_words": xtp[0],
        "xt_scales": xtp[1],
        "xo_words": xop[0],
        "xo_scales": xop[1],
        "w_words": wp[0],
        "w_scales": wp[1],
        "tg": (1.0 * n((R, Q))).astype(np.float32),
        "sg": (np.random.uniform(0.6, 1.6, (R, 1))).astype(np.float32),
        "bg": (np.random.uniform(-1.0, 1.0, (R, 1))).astype(np.float32),
        "wb_words": wbp[0],
        "wb_scales": wbp[1],
        "sx_words": sxp[0],
        "sx_scales": sxp[1],
        "ws_words": wsp[0],
        "ws_scales": wsp[1],
        "offs": striped(idx),
        "offs2": striped(idx2),
        "offs3": striped(idx3),
    }


def reference(xt_words, xt_scales, xo_words, xo_scales, w_words, w_scales, tg, sg, bg, wb_words, wb_scales, sx_words, sx_scales, ws_words, ws_scales, offs, offs2, offs3):
    idx = unstriped(offs)
    idx2 = unstriped(offs2)
    idx3 = unstriped(offs3)
    xtu = unpack_weight(xt_words, xt_scales, "e4m3")
    xou = unpack_weight(xo_words, xo_scales, "e2m1")
    wu = unpack_weight(w_words, w_scales, "e5m2")
    wbu = unpack_weight(wb_words, wb_scales, "e5m2")
    sxu = unpack_weight(sx_words, sx_scales, "e2m1")
    wsu = unpack_weight(ws_words, ws_scales, "e5m2")
    xtidxg = xtu[:, idx]
    a = wu.T @ xtidxg
    xoidx2g = xou[:, idx2]
    b = wu.T @ xoidx2g
    hid = np.maximum(a, b) * sigmoid(f64(tg)[:, idx3] * f64(sg) + f64(bg))
    hidq = mxq(hid, 0, "e4m3")
    y = wbu.T @ hidq + wsu.T @ sxu
    return y

@@ -1,0 +1,194 @@
+from contextlib import ExitStack
+
+import concourse.mybir as mybir
+
+K, T, Z, J, R, Q, N, L = 512, 1024, 1024, 256, 512, 1024, 256, 512
+FLOPS = 2 * J * (2 * K * R + R * N + L * N)
+
+F32 = mybir.dt.float32
+BF16 = mybir.dt.bfloat16
+I32 = mybir.dt.int32
+U32 = mybir.dt.uint32
+U16 = mybir.dt.uint16
+U8 = mybir.dt.uint8
+E4M3 = mybir.dt.float8_e4m3fn_x4
+E5M2 = mybir.dt.float8_e5m2_x4
+E2M1 = mybir.dt.float4_e2m1fn_x4
+ALU = mybir.AluOpType
+ACT = mybir.ActivationFunctionType
+
+P = 128
+PACK = 4
+ROWS = 16
+ROW0 = P - ROWS
+
+XT_S, XO_S, W_S, WB_S, WS_S, SX_S, S_END = 0, J, 2 * J, 2 * J + R, 2 * J + R + N, 2 * J + R + 2 * N, 3 * J + R + 2 * N
+
+
+def tile_list_oneforboth_tablegate_skip_plain_kernel(
+    tc, xt_words, xt_scales, xo_words, xo_scales, w_words, w_scales, tg, sg, bg,
+    wb_words, wb_scales, sx_words, sx_scales, ws_words, ws_scales, offs, offs2, offs3, out,
+):
+    nc = tc.nc
+    with ExitStack() as ctx:
+        lists = ctx.enter_context(tc.tile_pool(name="lists", bufs=1))
+        sb = ctx.enter_context(tc.tile_pool(name="sb", bufs=1))
+        ps = ctx.enter_context(tc.psum_pool(name="ps", bufs=1))
+
+        o1 = lists.tile([P, J // 16], U16, name="o1")
+        o2 = lists.tile([P, J // 16], U16, name="o2")
+        o3 = lists.tile([P, J // 16], U16, name="o3")
+
+        xt_s = sb.tile([P, T], U8, name="xt_s", align_bytes=64)
+        xo_s = sb.tile([P, Z], U8, name="xo_s", align_bytes=64)
+        w_s = sb.tile([P, R], U8, name="w_s", align_bytes=64)
+        staged = sb.tile([P, S_END], U8, name="staged", align_bytes=64)
+        planes = sb.tile([P, S_END], U8, name="planes", align_bytes=64)
+        xt_w = sb.tile([P, T], I32, name="xt_w", align_bytes=64)
+        xo_w = sb.tile([P, Z], U16, name="xo_w", align_bytes=64)
+        w_raw = sb.tile([P, R], I32, name="w_raw", tag="weights", align_bytes=64)
+        slope = sb.tile([P, PACK], F32, name="slope")
+        shift = sb.tile([P, PACK], F32, name="shift")
+        gates = [sb.tile([P, Q], F32, name="gates%d" % t) for t in range(PACK)]
+
+        for tile in (xt_s, xo_s, w_s):
+            nc.vector.memset(tile[0:ROW0, :].bitcast(I32), 0)
+        nc.vector.memset(planes[:].bitcast(I32), 0)
+
+        def load_rows(dst, src):
+            nc.sync.dma_start(out=dst.bitcast(I32), in_=src[0].bitcast(I32))
+
+        def as_words(words):
+            return words[0].rearrange("p n t -> p (n t)").bitcast(I32)
+
+        nc.sync.dma_start(out=xo_w[:].bitcast(I32), in_=xo_words[0].bitcast(I32))
+        nc.sync.dma_start(o1[:], offs)
+        load_rows(xt_s[ROW0:P, :], xt_scales)
+        nc.sync.dma_start(o2[:], offs2)
+        load_rows(xo_s[ROW0:P, :], xo_scales)
+        load_rows(w_s[ROW0:P, :], w_scales)
+        nc.sync.dma_start(out=w_raw[:], in_=as_words(w_words))
+        nc.sync.dma_start(out=xt_w[:], in_=as_words(xt_words))
+        load_rows(staged[ROW0:P, WB_S:WS_S], wb_scales)
+        load_rows(staged[ROW0:P, WS_S:SX_S], ws_scales)
+        load_rows(staged[ROW0:P, SX_S:S_END], sx_scales)
+        nc.sync.dma_start(o3[:], offs3)
+        nc.sync.dma_start(out=slope[:], in_=sg.rearrange("(p t) o -> p (t o)", t=PACK))
+        nc.sync.dma_start(out=shift[:], in_=bg.rearrange("(p t) o -> p (t o)", t=PACK))
+        tg_by_t = tg.rearrange("(p t) q -> t p q", t=PACK)
+        for t in range(PACK):
+            nc.sync.dma_start(out=gates[t][:], in_=tg_by_t[t])
+
+        xt_sg = sb.tile([P, J], U8, name="xt_sg", align_bytes=64)
+        xo_sg = sb.tile([P, J], U8, name="xo_sg", align_bytes=64)
+        nc.vector.tensor_copy(out=xt_sg[:], in_=xt_s[:].indirect(o1[:]))
+        nc.vector.tensor_copy(out=xo_sg[:], in_=xo_s[:].indirect(o2[:]))
+        nc.vector.tensor_copy(out=staged[:, XT_S:XO_S].bitcast(I32), in_=xt_sg[:].bitcast(I32))
+        nc.vector.tensor_copy(
+            out=staged[:, W_S:WB_S].rearrange("p (t m) -> p m t", t=PACK),
+            in_=w_s[:].rearrange("p (m t) -> p m t", t=PACK),
+        )
+        nc.vector.tensor_copy(out=staged[:, XO_S:W_S].bitcast(I32), in_=xo_sg[:].bitcast(I32))
+        for q in range(4):
+            nc.scalar.dma_start(
+                out=planes[32 * q : 32 * q + 4, :].bitcast(I32),
+                in_=staged[ROW0 + 4 * q : ROW0 + 4 * q + 4, :].bitcast(I32),
+            )
+
+        xt_g = sb.tile([P, J], U32, name="xt_g", align_bytes=64)
+        xo_g = sb.tile([P, J], U16, name="xo_g", align_bytes=64)
+        w_p = sb.tile([P, R], I32, name="w_p", align_bytes=64)
+        nc.vector.tensor_copy(
+            out=w_p[:].rearrange("p (t m) -> p m t", t=PACK),
+            in_=w_raw[:].rearrange("p (m t) -> p m t", t=PACK),
+        )
+        nc.vector.tensor_copy(out=xt_g[:], in_=xt_w[:].bitcast(U32).indirect(o1[:]))
+        nc.vector.tensor_copy(out=xo_g[:], in_=xo_w[:].indirect(o2[:]))
+
+        late = sb.tile([P, 2 * N + J // 2], I32, name="late", tag="weights", align_bytes=64)
+        wb_w, ws_w, sx_w = late[:, 0:N], late[:, N : 2 * N], late[:, 2 * N : 2 * N + J // 2]
+        nc.sync.dma_start(out=ws_w, in_=as_words(ws_words))
+        nc.sync.dma_start(out=sx_w, in_=sx_words[0].bitcast(I32))
+        nc.sync.dma_start(out=wb_w, in_=as_words(wb_words))
+
+        gate = sb.tile([P, PACK, J], F32, name="gate")
+        for t in range(PACK):
+            nc.scalar.activation(
+                out=gate[:, t, :], in_=gates[t][:].indirect(o3[:]), func=ACT.Sigmoid,
+                bias=shift[:, t : t + 1], scale=slope[:, t : t + 1],
+            )
+
+        a_sb = sb.tile([P, PACK, J], F32, name="a_sb")
+        larger = sb.tile([P, PACK, J], F32, name="larger")
+        hid = sb.tile([P, J, PACK], BF16, name="hid", align_bytes=64)
+
+        def first_stage(ts):
+            width = len(ts) * J
+            a_ps = ps.tile([P, width], F32, name="a_ps%d" % ts[0])
+            b_ps = ps.tile([P, width], F32, name="b_ps%d" % ts[0])
+            for bank, words, fmt, s0 in ((a_ps, xt_g, E4M3, XT_S), (b_ps, xo_g, E2M1, XO_S)):
+                for i, t in enumerate(ts):
+                    nc.tensor.matmul_mx(
+                        out=bank[:, i * J : (i + 1) * J],
+                        lhsT=w_p[:, t * P : (t + 1) * P].bitcast(E5M2),
+                        lhsT_scale=planes[:, W_S + t * P : W_S + (t + 1) * P],
+                        rhs=words[:].bitcast(fmt),
+                        rhs_scale=planes[:, s0 : s0 + J],
+                        start=True, stop=True,
+                    )
+            lo, hi = ts[0], ts[-1] + 1
+            a_flat = a_sb[:, lo:hi, :].rearrange("p t j -> p (t j)")
+            nc.scalar.copy(out=a_flat, in_=a_ps[:])
+            nc.vector.tensor_tensor(
+                out=larger[:, lo:hi, :].rearrange("p t j -> p (t j)"), in0=b_ps[:], in1=a_flat, op=ALU.max
+            )
+
+        def gated(lo, cols):
+            nc.vector.tensor_tensor(
+                out=hid[:, cols, lo : lo + 2],
+                in0=larger[:, lo : lo + 2, cols].rearrange("p t j -> p j t"),
+                in1=gate[:, lo : lo + 2, cols].rearrange("p t j -> p j t"),
+                op=ALU.mult,
+            )
+
+        first_stage([0, 1])
+        gated(0, slice(0, J))
+        first_stage([2])
+        first_stage([3])
+        halves = [slice(0, J // 2), slice(J // 2, J)]
+        for cols in halves:
+            gated(2, cols)
+
+        hid_w = sb.tile([P, J], U32, name="hid_w", align_bytes=64)
+        hid_s = sb.tile([P, J], U8, name="hid_s", align_bytes=64)
+        for cols in halves:
+            nc.vector.quantize_mx(
+                out=hid_w[:, cols].bitcast(E4M3), scales=hid_s[:, cols], in_=hid[:, cols, :].rearrange("p j t -> p (j t)")
+            )
+
+        y_ps = [ps.tile([P, J], F32, name="y_ps%d" % h) for h in range(N // P)]
+        for h in range(N // P):
+            nc.tensor.matmul_mx(
+                out=y_ps[h][:],
+                lhsT=ws_w[:, h * P : (h + 1) * P].bitcast(E5M2),
+                lhsT_scale=planes[:, WS_S + h * P : WS_S + (h + 1) * P],
+                rhs=sx_w.bitcast(E2M1),
+                rhs_scale=planes[:, SX_S:S_END],
+                start=True, stop=False,
+            )
+        for c, cols in enumerate(halves):
+            for h in range(N // P):
+                nc.tensor.matmul_mx(
+                    out=y_ps[h][:, cols],
+                    lhsT=wb_w[:, h * P : (h + 1) * P].bitcast(E5M2),
+                    lhsT_scale=planes[:, WB_S + h * P : WB_S + (h + 1) * P],
+                    rhs=hid_w[:, cols].bitcast(E4M3),
+                    rhs_scale=hid_s[:, cols],
+                    start=False, stop=(c == len(halves) - 1),
+                )
+        y0 = sb.tile([P, J], F32, name="y0")
+        y1 = sb.tile([P, J], F32, name="y1")
+        nc.scalar.copy(out=y0[:], in_=y_ps[0][:])
+        nc.scalar.dma_start(out=out[0:P, :], in_=y0[:])
+        nc.vector.tensor_copy(out=y1[:], in_=y_ps[1][:])
+        nc.sync.dma_start(out=out[P : 2 * P, :], in_=y1[:])

@@ -22,7 +22,7 @@ PACK = 4
 ROWS = 16
 ROW0 = P - ROWS
 
-XT_S, XO_S, W_S, WB_S, WS_S, SX_S, S_END = 0, J, 2 * J, 2 * J + R, 2 * J + R + N, 2 * J + R + 2 * N, 3 * J + R + 2 * N
+XT_S, XO_S, W_S, WS_S, SX_S, S_END = 0, J, 2 * J, 2 * J + R, 2 * J + R + N, 3 * J + R + N
 
 
 def tile_list_oneforboth_tablegate_skip_plain_kernel(
@@ -44,56 +44,63 @@ def tile_list_oneforboth_tablegate_skip_plain_kernel(
         w_s = sb.tile([P, R], U8, name="w_s", align_bytes=64)
         staged = sb.tile([P, S_END], U8, name="staged", align_bytes=64)
         planes = sb.tile([P, S_END], U8, name="planes", align_bytes=64)
-        xt_w = sb.tile([P, T], I32, name="xt_w", align_bytes=64)
-        xo_w = sb.tile([P, Z], U16, name="xo_w", align_bytes=64)
-        w_raw = sb.tile([P, R], I32, name="w_raw", tag="weights", align_bytes=64)
+        xt_w = sb.tile([P, T], I32, name="xt_w", tag="reuse3", align_bytes=64)
+        xo_w = sb.tile([P, Z], U16, name="xo_w", tag="reuse4", align_bytes=64)
+        w_raw = sb.tile([P, R], I32, name="w_raw", align_bytes=64)
         slope = sb.tile([P, PACK], F32, name="slope")
         shift = sb.tile([P, PACK], F32, name="shift")
-        gates = [sb.tile([P, Q], F32, name="gates%d" % t) for t in range(PACK)]
 
         for tile in (xt_s, xo_s, w_s):
             nc.vector.memset(tile[0:ROW0, :].bitcast(I32), 0)
         nc.vector.memset(planes[:].bitcast(I32), 0)
 
-        def load_rows(dst, src):
-            nc.sync.dma_start(out=dst.bitcast(I32), in_=src[0].bitcast(I32))
+        def load_rows(dst, src, queue=nc.sync):
+            queue.dma_start(out=dst.bitcast(I32), in_=src[0].bitcast(I32))
 
         def as_words(words):
             return words[0].rearrange("p n t -> p (n t)").bitcast(I32)
 
-        nc.sync.dma_start(out=xo_w[:].bitcast(I32), in_=xo_words[0].bitcast(I32))
+        tg_by_t = tg.rearrange("(p t) q -> t p q", t=PACK)
+        gates = []
+
+        def load_gates(t, tag):
+            tile = sb.tile([P, Q], F32, name="gates%d" % t, tag=tag, align_bytes=64)
+            nc.sync.dma_start(out=tile[:], in_=tg_by_t[t])
+            gates.append(tile)
+
         nc.sync.dma_start(o1[:], offs)
-        load_rows(xt_s[ROW0:P, :], xt_scales)
+        load_rows(xt_s[ROW0:P, :], xt_scales, nc.scalar)
         nc.sync.dma_start(o2[:], offs2)
-        load_rows(xo_s[ROW0:P, :], xo_scales)
-        load_rows(w_s[ROW0:P, :], w_scales)
-        nc.sync.dma_start(out=w_raw[:], in_=as_words(w_words))
-        nc.sync.dma_start(out=xt_w[:], in_=as_words(xt_words))
-        load_rows(staged[ROW0:P, WB_S:WS_S], wb_scales)
+        load_rows(xo_s[ROW0:P, :], xo_scales, nc.scalar)
         load_rows(staged[ROW0:P, WS_S:SX_S], ws_scales)
+        load_rows(w_s[ROW0:P, :], w_scales, nc.scalar)
+        nc.sync.dma_start(out=xt_w[:], in_=as_words(xt_words))
+        nc.sync.dma_start(out=w_raw[:], in_=as_words(w_words))
+        nc.sync.dma_start(out=xo_w[:].bitcast(I32), in_=xo_words[0].bitcast(I32))
         load_rows(staged[ROW0:P, SX_S:S_END], sx_scales)
         nc.sync.dma_start(o3[:], offs3)
         nc.sync.dma_start(out=slope[:], in_=sg.rearrange("(p t) o -> p (t o)", t=PACK))
         nc.sync.dma_start(out=shift[:], in_=bg.rearrange("(p t) o -> p (t o)", t=PACK))
-        tg_by_t = tg.rearrange("(p t) q -> t p q", t=PACK)
-        for t in range(PACK):
-            nc.sync.dma_start(out=gates[t][:], in_=tg_by_t[t])
+        load_gates(0, "gates0")
+        load_gates(1, "gates1")
 
         xt_sg = sb.tile([P, J], U8, name="xt_sg", align_bytes=64)
-        xo_sg = sb.tile([P, J], U8, name="xo_sg", align_bytes=64)
+        xo_sg = sb.tile([P, J], U8, name="xo_sg", tag="reuse1", align_bytes=64)
         nc.vector.tensor_copy(out=xt_sg[:], in_=xt_s[:].indirect(o1[:]))
         nc.vector.tensor_copy(out=xo_sg[:], in_=xo_s[:].indirect(o2[:]))
         nc.vector.tensor_copy(out=staged[:, XT_S:XO_S].bitcast(I32), in_=xt_sg[:].bitcast(I32))
         nc.vector.tensor_copy(
-            out=staged[:, W_S:WB_S].rearrange("p (t m) -> p m t", t=PACK),
+            out=staged[:, W_S:WS_S].rearrange("p (t m) -> p m t", t=PACK),
             in_=w_s[:].rearrange("p (m t) -> p m t", t=PACK),
         )
         nc.vector.tensor_copy(out=staged[:, XO_S:W_S].bitcast(I32), in_=xo_sg[:].bitcast(I32))
         for q in range(4):
-            nc.scalar.dma_start(
+            nc.sync.dma_start(
                 out=planes[32 * q : 32 * q + 4, :].bitcast(I32),
                 in_=staged[ROW0 + 4 * q : ROW0 + 4 * q + 4, :].bitcast(I32),
             )
+
+        load_gates(2, "reuse1")
 
         xt_g = sb.tile([P, J], U32, name="xt_g", align_bytes=64)
         xo_g = sb.tile([P, J], U16, name="xo_g", align_bytes=64)
@@ -103,13 +110,19 @@ def tile_list_oneforboth_tablegate_skip_plain_kernel(
             in_=w_raw[:].rearrange("p (m t) -> p m t", t=PACK),
         )
         nc.vector.tensor_copy(out=xt_g[:], in_=xt_w[:].bitcast(U32).indirect(o1[:]))
+        load_gates(3, "reuse3")
         nc.vector.tensor_copy(out=xo_g[:], in_=xo_w[:].indirect(o2[:]))
-
-        late = sb.tile([P, 2 * N + J // 2], I32, name="late", tag="weights", align_bytes=64)
+        late = sb.tile([P, 2 * N + J // 2], I32, name="late", tag="reuse4", align_bytes=64)
         wb_w, ws_w, sx_w = late[:, 0:N], late[:, N : 2 * N], late[:, 2 * N : 2 * N + J // 2]
         nc.sync.dma_start(out=ws_w, in_=as_words(ws_words))
         nc.sync.dma_start(out=sx_w, in_=sx_words[0].bitcast(I32))
         nc.sync.dma_start(out=wb_w, in_=as_words(wb_words))
+        wb_s = sb.tile([P, N], U8, name="wb_s", tag="staged", align_bytes=64)
+        nc.vector.memset(wb_s[:].bitcast(I32), 0)
+        for q in range(4):
+            nc.sync.dma_start(
+                out=wb_s[32 * q : 32 * q + 4, :].bitcast(I32), in_=wb_scales[0, 4 * q : 4 * q + 4, :].bitcast(I32)
+            )
 
         gate = sb.tile([P, PACK, J], F32, name="gate")
         for t in range(PACK):
@@ -118,46 +131,40 @@ def tile_list_oneforboth_tablegate_skip_plain_kernel(
                 bias=shift[:, t : t + 1], scale=slope[:, t : t + 1],
             )
 
-        a_sb = sb.tile([P, PACK, J], F32, name="a_sb")
         larger = sb.tile([P, PACK, J], F32, name="larger")
         hid = sb.tile([P, J, PACK], BF16, name="hid", align_bytes=64)
 
-        def first_stage(ts):
-            width = len(ts) * J
-            a_ps = ps.tile([P, width], F32, name="a_ps%d" % ts[0])
-            b_ps = ps.tile([P, width], F32, name="b_ps%d" % ts[0])
-            for bank, words, fmt, s0 in ((a_ps, xt_g, E4M3, XT_S), (b_ps, xo_g, E2M1, XO_S)):
-                for i, t in enumerate(ts):
-                    nc.tensor.matmul_mx(
-                        out=bank[:, i * J : (i + 1) * J],
-                        lhsT=w_p[:, t * P : (t + 1) * P].bitcast(E5M2),
-                        lhsT_scale=planes[:, W_S + t * P : W_S + (t + 1) * P],
-                        rhs=words[:].bitcast(fmt),
-                        rhs_scale=planes[:, s0 : s0 + J],
-                        start=True, stop=True,
-                    )
-            lo, hi = ts[0], ts[-1] + 1
-            a_flat = a_sb[:, lo:hi, :].rearrange("p t j -> p (t j)")
-            nc.scalar.copy(out=a_flat, in_=a_ps[:])
-            nc.vector.tensor_tensor(
-                out=larger[:, lo:hi, :].rearrange("p t j -> p (t j)"), in0=b_ps[:], in1=a_flat, op=ALU.max
+        def product(dst, t, words, fmt, s0):
+            nc.tensor.matmul_mx(
+                out=dst,
+                lhsT=w_p[:, t * P : (t + 1) * P].bitcast(E5M2),
+                lhsT_scale=planes[:, W_S + t * P : W_S + (t + 1) * P],
+                rhs=words[:].bitcast(fmt),
+                rhs_scale=planes[:, s0 : s0 + J],
+                start=True, stop=True,
             )
 
-        def gated(lo, cols):
+        def first_stage_in_one_bank(t):
+            both = ps.tile([P, 2, J], F32, name="both%d" % t)
+            product(both[:, 0, :], t, xt_g, E4M3, XT_S)
+            product(both[:, 1, :], t, xo_g, E2M1, XO_S)
+            nc.vector.tensor_reduce(
+                out=larger[:, t, :], in_=both[:].rearrange("p s j -> p j s"), op=ALU.max, axis=mybir.AxisListType.X
+            )
+
+        def gated(cols):
             nc.vector.tensor_tensor(
-                out=hid[:, cols, lo : lo + 2],
-                in0=larger[:, lo : lo + 2, cols].rearrange("p t j -> p j t"),
-                in1=gate[:, lo : lo + 2, cols].rearrange("p t j -> p j t"),
+                out=hid[:, cols, :].rearrange("p (c i) t -> p c t i", i=4),
+                in0=larger[:, :, cols].rearrange("p t (c i) -> p c t i", i=4),
+                in1=gate[:, :, cols].rearrange("p t (c i) -> p c t i", i=4),
                 op=ALU.mult,
             )
 
-        first_stage([0, 1])
-        gated(0, slice(0, J))
-        first_stage([2])
-        first_stage([3])
+        for t in range(PACK):
+            first_stage_in_one_bank(t)
         halves = [slice(0, J // 2), slice(J // 2, J)]
         for cols in halves:
-            gated(2, cols)
+            gated(cols)
 
         hid_w = sb.tile([P, J], U32, name="hid_w", align_bytes=64)
         hid_s = sb.tile([P, J], U8, name="hid_s", align_bytes=64)
@@ -166,29 +173,36 @@ def tile_list_oneforboth_tablegate_skip_plain_kernel(
                 out=hid_w[:, cols].bitcast(E4M3), scales=hid_s[:, cols], in_=hid[:, cols, :].rearrange("p j t -> p (j t)")
             )
 
-        y_ps = [ps.tile([P, J], F32, name="y_ps%d" % h) for h in range(N // P)]
-        for h in range(N // P):
-            nc.tensor.matmul_mx(
-                out=y_ps[h][:],
-                lhsT=ws_w[:, h * P : (h + 1) * P].bitcast(E5M2),
-                lhsT_scale=planes[:, WS_S + h * P : WS_S + (h + 1) * P],
-                rhs=sx_w.bitcast(E2M1),
-                rhs_scale=planes[:, SX_S:S_END],
-                start=True, stop=False,
-            )
+        first = ps.tile([P, 2, J // 2], F32, name="first")
+        second = [ps.tile([P, J // 2], F32, name="second%d" % h) for h in range(2)]
+        sums = [[first[:, 0, :], first[:, 1, :]], [second[0][:], second[1][:]]]
+        sx_b = sx_w.bitcast(E2M1)
         for c, cols in enumerate(halves):
-            for h in range(N // P):
+            for h in range(2):
                 nc.tensor.matmul_mx(
-                    out=y_ps[h][:, cols],
+                    out=sums[c][h],
+                    lhsT=ws_w[:, h * P : (h + 1) * P].bitcast(E5M2),
+                    lhsT_scale=planes[:, WS_S + h * P : WS_S + (h + 1) * P],
+                    rhs=sx_b[:, cols],
+                    rhs_scale=planes[:, SX_S + cols.start : SX_S + cols.stop],
+                    start=(c == 1 or h == 0), stop=False,
+                )
+        for c, cols in enumerate(halves):
+            for h in range(2):
+                nc.tensor.matmul_mx(
+                    out=sums[c][h],
                     lhsT=wb_w[:, h * P : (h + 1) * P].bitcast(E5M2),
-                    lhsT_scale=planes[:, WB_S + h * P : WB_S + (h + 1) * P],
+                    lhsT_scale=wb_s[:, h * P : (h + 1) * P],
                     rhs=hid_w[:, cols].bitcast(E4M3),
                     rhs_scale=hid_s[:, cols],
-                    start=False, stop=(c == len(halves) - 1),
+                    start=False, stop=(c == 1 or h == 1),
                 )
-        y0 = sb.tile([P, J], F32, name="y0")
-        y1 = sb.tile([P, J], F32, name="y1")
-        nc.scalar.copy(out=y0[:], in_=y_ps[0][:])
-        nc.scalar.dma_start(out=out[0:P, :], in_=y0[:])
-        nc.vector.tensor_copy(out=y1[:], in_=y_ps[1][:])
-        nc.sync.dma_start(out=out[P : 2 * P, :], in_=y1[:])
+        y0 = sb.tile([P, 2, J // 2], F32, name="y0")
+        y1 = sb.tile([P, J // 2], F32, name="y1")
+        y2 = sb.tile([P, J // 2], F32, name="y2")
+        nc.scalar.copy(out=y0[:], in_=first[:])
+        nc.sync.dma_start(out=out[:, halves[0]].rearrange("(h p) j -> p h j", p=P), in_=y0[:])
+        nc.scalar.copy(out=y1[:], in_=second[0][:])
+        nc.scalar.dma_start(out=out[0:P, halves[1]], in_=y1[:])
+        nc.vector.tensor_copy(out=y2[:], in_=second[1][:])
+        nc.sync.dma_start(out=out[P : 2 * P, halves[1]], in_=y2[:])

from contextlib import ExitStack

import concourse.mybir as mybir

K, T, Z, J, R, Q, N, L = 512, 1024, 1024, 256, 512, 1024, 256, 512
FLOPS = 2 * J * (2 * K * R + R * N + L * N)

F32 = mybir.dt.float32
BF16 = mybir.dt.bfloat16
I32 = mybir.dt.int32
U32 = mybir.dt.uint32
U16 = mybir.dt.uint16
U8 = mybir.dt.uint8
E4M3 = mybir.dt.float8_e4m3fn_x4
E5M2 = mybir.dt.float8_e5m2_x4
E2M1 = mybir.dt.float4_e2m1fn_x4
ALU = mybir.AluOpType
ACT = mybir.ActivationFunctionType

P = 128
PACK = 4
ROWS = 16
ROW0 = P - ROWS

XT_S, XO_S, W_S, WS_S, SX_S, S_END = 0, J, 2 * J, 2 * J + R, 2 * J + R + N, 3 * J + R + N


def tile_list_oneforboth_tablegate_skip_plain_kernel(
    tc, xt_words, xt_scales, xo_words, xo_scales, w_words, w_scales, tg, sg, bg,
    wb_words, wb_scales, sx_words, sx_scales, ws_words, ws_scales, offs, offs2, offs3, out,
):
    nc = tc.nc
    with ExitStack() as ctx:
        lists = ctx.enter_context(tc.tile_pool(name="lists", bufs=1))
        sb = ctx.enter_context(tc.tile_pool(name="sb", bufs=1))
        ps = ctx.enter_context(tc.psum_pool(name="ps", bufs=1))

        o1 = lists.tile([P, J // 16], U16, name="o1")
        o2 = lists.tile([P, J // 16], U16, name="o2")
        o3 = lists.tile([P, J // 16], U16, name="o3")

        xt_s = sb.tile([P, T], U8, name="xt_s", align_bytes=64)
        xo_s = sb.tile([P, Z], U8, name="xo_s", align_bytes=64)
        w_s = sb.tile([P, R], U8, name="w_s", align_bytes=64)
        staged = sb.tile([P, S_END], U8, name="staged", align_bytes=64)
        planes = sb.tile([P, S_END], U8, name="planes", align_bytes=64)
        xt_w = sb.tile([P, T], I32, name="xt_w", tag="reuse3", align_bytes=64)
        xo_w = sb.tile([P, Z], U16, name="xo_w", tag="reuse4", align_bytes=64)
        w_raw = sb.tile([P, R], I32, name="w_raw", align_bytes=64)
        slope = sb.tile([P, PACK], F32, name="slope")
        shift = sb.tile([P, PACK], F32, name="shift")

        for tile in (xt_s, xo_s, w_s):
            nc.vector.memset(tile[0:ROW0, :].bitcast(I32), 0)
        nc.vector.memset(planes[:].bitcast(I32), 0)

        def load_rows(dst, src, queue=nc.sync):
            queue.dma_start(out=dst.bitcast(I32), in_=src[0].bitcast(I32))

        def as_words(words):
            return words[0].rearrange("p n t -> p (n t)").bitcast(I32)

        tg_by_t = tg.rearrange("(p t) q -> t p q", t=PACK)
        gates = []

        def load_gates(t, tag):
            tile = sb.tile([P, Q], F32, name="gates%d" % t, tag=tag, align_bytes=64)
            nc.sync.dma_start(out=tile[:], in_=tg_by_t[t])
            gates.append(tile)

        nc.sync.dma_start(o1[:], offs)
        load_rows(xt_s[ROW0:P, :], xt_scales, nc.scalar)
        nc.sync.dma_start(o2[:], offs2)
        load_rows(xo_s[ROW0:P, :], xo_scales, nc.scalar)
        load_rows(staged[ROW0:P, WS_S:SX_S], ws_scales)
        load_rows(w_s[ROW0:P, :], w_scales, nc.scalar)
        nc.sync.dma_start(out=xt_w[:], in_=as_words(xt_words))
        nc.sync.dma_start(out=w_raw[:], in_=as_words(w_words))
        nc.sync.dma_start(out=xo_w[:].bitcast(I32), in_=xo_words[0].bitcast(I32))
        load_rows(staged[ROW0:P, SX_S:S_END], sx_scales)
        nc.sync.dma_start(o3[:], offs3)
        nc.sync.dma_start(out=slope[:], in_=sg.rearrange("(p t) o -> p (t o)", t=PACK))
        nc.sync.dma_start(out=shift[:], in_=bg.rearrange("(p t) o -> p (t o)", t=PACK))
        load_gates(0, "gates0")
        load_gates(1, "gates1")

        xt_sg = sb.tile([P, J], U8, name="xt_sg", align_bytes=64)
        xo_sg = sb.tile([P, J], U8, name="xo_sg", tag="reuse1", align_bytes=64)
        nc.vector.tensor_copy(out=xt_sg[:], in_=xt_s[:].indirect(o1[:]))
        nc.vector.tensor_copy(out=xo_sg[:], in_=xo_s[:].indirect(o2[:]))
        nc.vector.tensor_copy(out=staged[:, XT_S:XO_S].bitcast(I32), in_=xt_sg[:].bitcast(I32))
        nc.vector.tensor_copy(
            out=staged[:, W_S:WS_S].rearrange("p (t m) -> p m t", t=PACK),
            in_=w_s[:].rearrange("p (m t) -> p m t", t=PACK),
        )
        nc.vector.tensor_copy(out=staged[:, XO_S:W_S].bitcast(I32), in_=xo_sg[:].bitcast(I32))
        for q in range(4):
            nc.sync.dma_start(
                out=planes[32 * q : 32 * q + 4, :].bitcast(I32),
                in_=staged[ROW0 + 4 * q : ROW0 + 4 * q + 4, :].bitcast(I32),
            )

        load_gates(2, "reuse1")

        xt_g = sb.tile([P, J], U32, name="xt_g", align_bytes=64)
        xo_g = sb.tile([P, J], U16, name="xo_g", align_bytes=64)
        w_p = sb.tile([P, R], I32, name="w_p", align_bytes=64)
        nc.vector.tensor_copy(
            out=w_p[:].rearrange("p (t m) -> p m t", t=PACK),
            in_=w_raw[:].rearrange("p (m t) -> p m t", t=PACK),
        )
        nc.vector.tensor_copy(out=xt_g[:], in_=xt_w[:].bitcast(U32).indirect(o1[:]))
        load_gates(3, "reuse3")
        nc.vector.tensor_copy(out=xo_g[:], in_=xo_w[:].indirect(o2[:]))
        late = sb.tile([P, 2 * N + J // 2], I32, name="late", tag="reuse4", align_bytes=64)
        wb_w, ws_w, sx_w = late[:, 0:N], late[:, N : 2 * N], late[:, 2 * N : 2 * N + J // 2]
        nc.sync.dma_start(out=ws_w, in_=as_words(ws_words))
        nc.sync.dma_start(out=sx_w, in_=sx_words[0].bitcast(I32))
        nc.sync.dma_start(out=wb_w, in_=as_words(wb_words))
        wb_s = sb.tile([P, N], U8, name="wb_s", tag="staged", align_bytes=64)
        nc.vector.memset(wb_s[:].bitcast(I32), 0)
        for q in range(4):
            nc.sync.dma_start(
                out=wb_s[32 * q : 32 * q + 4, :].bitcast(I32), in_=wb_scales[0, 4 * q : 4 * q + 4, :].bitcast(I32)
            )

        gate = sb.tile([P, PACK, J], F32, name="gate")
        for t in range(PACK):
            nc.scalar.activation(
                out=gate[:, t, :], in_=gates[t][:].indirect(o3[:]), func=ACT.Sigmoid,
                bias=shift[:, t : t + 1], scale=slope[:, t : t + 1],
            )

        larger = sb.tile([P, PACK, J], F32, name="larger")
        hid = sb.tile([P, J, PACK], BF16, name="hid", align_bytes=64)

        def product(dst, t, words, fmt, s0):
            nc.tensor.matmul_mx(
                out=dst,
                lhsT=w_p[:, t * P : (t + 1) * P].bitcast(E5M2),
                lhsT_scale=planes[:, W_S + t * P : W_S + (t + 1) * P],
                rhs=words[:].bitcast(fmt),
                rhs_scale=planes[:, s0 : s0 + J],
                start=True, stop=True,
            )

        def first_stage_in_one_bank(t):
            both = ps.tile([P, 2, J], F32, name="both%d" % t)
            product(both[:, 0, :], t, xt_g, E4M3, XT_S)
            product(both[:, 1, :], t, xo_g, E2M1, XO_S)
            nc.vector.tensor_reduce(
                out=larger[:, t, :], in_=both[:].rearrange("p s j -> p j s"), op=ALU.max, axis=mybir.AxisListType.X
            )

        def gated(cols):
            nc.vector.tensor_tensor(
                out=hid[:, cols, :].rearrange("p (c i) t -> p c t i", i=4),
                in0=larger[:, :, cols].rearrange("p t (c i) -> p c t i", i=4),
                in1=gate[:, :, cols].rearrange("p t (c i) -> p c t i", i=4),
                op=ALU.mult,
            )

        for t in range(PACK):
            first_stage_in_one_bank(t)
        halves = [slice(0, J // 2), slice(J // 2, J)]
        for cols in halves:
            gated(cols)

        hid_w = sb.tile([P, J], U32, name="hid_w", align_bytes=64)
        hid_s = sb.tile([P, J], U8, name="hid_s", align_bytes=64)
        for cols in halves:
            nc.vector.quantize_mx(
                out=hid_w[:, cols].bitcast(E4M3), scales=hid_s[:, cols], in_=hid[:, cols, :].rearrange("p j t -> p (j t)")
            )

        first = ps.tile([P, 2, J // 2], F32, name="first")
        second = [ps.tile([P, J // 2], F32, name="second%d" % h) for h in range(2)]
        sums = [[first[:, 0, :], first[:, 1, :]], [second[0][:], second[1][:]]]
        sx_b = sx_w.bitcast(E2M1)
        for c, cols in enumerate(halves):
            for h in range(2):
                nc.tensor.matmul_mx(
                    out=sums[c][h],
                    lhsT=ws_w[:, h * P : (h + 1) * P].bitcast(E5M2),
                    lhsT_scale=planes[:, WS_S + h * P : WS_S + (h + 1) * P],
                    rhs=sx_b[:, cols],
                    rhs_scale=planes[:, SX_S + cols.start : SX_S + cols.stop],
                    start=(c == 1 or h == 0), stop=False,
                )
        for c, cols in enumerate(halves):
            for h in range(2):
                nc.tensor.matmul_mx(
                    out=sums[c][h],
                    lhsT=wb_w[:, h * P : (h + 1) * P].bitcast(E5M2),
                    lhsT_scale=wb_s[:, h * P : (h + 1) * P],
                    rhs=hid_w[:, cols].bitcast(E4M3),
                    rhs_scale=hid_s[:, cols],
                    start=False, stop=(c == 1 or h == 1),
                )
        y0 = sb.tile([P, 2, J // 2], F32, name="y0")
        y1 = sb.tile([P, J // 2], F32, name="y1")
        y2 = sb.tile([P, J // 2], F32, name="y2")
        nc.scalar.copy(out=y0[:], in_=first[:])
        nc.sync.dma_start(out=out[:, halves[0]].rearrange("(h p) j -> p h j", p=P), in_=y0[:])
        nc.scalar.copy(out=y1[:], in_=second[0][:])
        nc.scalar.dma_start(out=out[0:P, halves[1]], in_=y1[:])
        nc.vector.tensor_copy(out=y2[:], in_=second[1][:])
        nc.sync.dma_start(out=out[P : 2 * P, halves[1]], in_=y2[:])
